import numpy as np
import ml_dtypes


def mxq(x, axis, fmt="e4m3"):
    dtype, down = {"e4m3": (ml_dtypes.float8_e4m3fn, 7), "e5m2": (ml_dtypes.float8_e5m2, 14)}[fmt]
    v = np.moveaxis(np.asarray(x, np.float32).astype(ml_dtypes.bfloat16).astype(np.float64), axis, -1)
    blocks = v.reshape(v.shape[:-1] + (-1, 32))
    amax = np.abs(blocks).max(-1, keepdims=True)
    byte = np.maximum(np.where(amax > 0, np.frexp(amax)[1] - 1 + 127, 0) - down, 1)
    scale = np.exp2(byte - 127.0)
    codes = (blocks / scale).astype(np.float32).astype(dtype).astype(np.float64)
    return np.moveaxis((codes * scale).reshape(v.shape), -1, axis)


WIDE = False


def mx_kscale(k):
    if not WIDE:
        return np.ones(k)
    levels = np.array([10, -10, 5, -5, 0])
    if k % 512:
        return np.exp2(np.random.permutation(np.resize(levels, k // 32))).repeat(32)
    a = np.empty((k // 512, 16))
    for p in range(k // 512):
        a[p, :8] = np.random.permutation(np.resize(levels, 8))
        for g in range(8):
            far = levels[np.abs(levels - a[p, g]) >= 10]
            a[p, g + 8] = far[np.random.randint(len(far))]
    return np.exp2(a.ravel()).repeat(32)


def f64(x):
    return np.asarray(x).astype(np.float64)


def striped(idx):
    return np.tile(idx.reshape(-1, 16).T, (8, 1)).astype(np.uint16)


def unstriped(offs):
    return offs[:16].T.reshape(-1).astype(np.int64)


K, T, E, C, N = 2560, 512, 2, 256, 128


def by_expert(wq, xq):
    return np.concatenate([wq[e].T @ xq[:, e * C:(e + 1) * C] for e in range(E)], axis=1)


def setup_inputs():
    n = np.random.standard_normal
    s = mx_kscale(K)[:, None]
    return {
        "xT": (n((K, T)) * s).astype(np.float32),
        "w": (n((E, K, N)) / np.sqrt(K) / s[None]).astype(np.float32),
        "gate": np.tile(np.random.uniform(0.2, 1.0, E * C), (N, 1)).astype(np.float32),
        "offs": striped(np.random.permutation(T)[:E * C]),
        "dst": striped(np.random.permutation(T)[:E * C]),
    }


def reference(xT, w, gate, offs, dst):
    idx = unstriped(offs)
    xq = mxq(f64(xT)[:, idx], 0, "e4m3")
    y = by_expert(mxq(f64(w), 1, "e4m3"), xq)
    out = np.zeros((N, T))
    out[:, unstriped(dst)] = f64(gate) * y
    return out

@@ -1,0 +1,193 @@
+from contextlib import ExitStack
+
+import concourse.mybir as mybir
+
+K, T, E, C, N = 2560, 512, 2, 256, 128
+FLOPS = 2 * K * N * E * C
+
+F32 = mybir.dt.float32
+BF16 = mybir.dt.bfloat16
+U32 = mybir.dt.uint32
+I32 = mybir.dt.int32
+U16 = mybir.dt.uint16
+U8 = mybir.dt.uint8
+FP8X4 = mybir.dt.float8_e4m3fn_x4
+MULT = mybir.AluOpType.mult
+
+P = 128
+PASSES = K // 512
+
+
+def tile_moe_two_lin_none_kernel(tc, xT, w, gate, offs, dst, out):
+    nc = tc.nc
+    with ExitStack() as ctx:
+        keep = ctx.enter_context(tc.tile_pool(name="keep", bufs=1))
+        psum = ctx.enter_context(tc.psum_pool(name="psum", bufs=1))
+
+        offs_sb = keep.tile([P, E * C // 16], U16, name="offs_sb")
+        dst_sb = keep.tile([P, E * C // 16], U16, name="dst_sb")
+        gate_sb = keep.tile([P, E * C], F32, name="gate_sb")
+
+        xs = keep.tile([P, 2 * T], U8, name="xs", align_bytes=64)
+        nc.gpsimd.memset(xs[:], 0)
+        xg_s = [keep.tile([P, E * C], U8, name=f"xgs{b}", align_bytes=64) for b in range(2)]
+
+        chunks = {}
+
+        def load_w(e, a0, n):
+            raw = keep.tile([P, n, 4, N], F32, name=f"wraw{e}_{a0}")
+            nc.sync.dma_start(
+                out=raw[:],
+                in_=w[e, a0 * 512 : (a0 + n) * 512, :].rearrange("(a p j) n -> p a j n", p=P, j=4),
+            )
+            chunks[e, a0] = raw
+
+        x_raw = []
+
+        def load_x(a, cuts):
+            pieces = []
+            for lo, hi in cuts:
+                raw = keep.tile([P, 4, hi - lo], F32, name=f"xraw{a}_{lo}")
+                nc.sync.dma_start(
+                    out=raw[:], in_=xT[a * 512 : (a + 1) * 512, lo:hi].rearrange("(p j) t -> p j t", j=4)
+                )
+                pieces.append((lo, hi, raw))
+            x_raw.append(pieces)
+
+        load_x(0, [(0, 256), (256, 512)])
+        nc.sync.dma_start(offs_sb[:], offs)
+        for a in range(1, PASSES):
+            load_x(a, [(0, T)])
+        load_w(0, 0, 3)
+        load_w(0, 3, 2)
+        nc.sync.dma_start(dst_sb[:], dst)
+        nc.sync.dma_start(out=gate_sb[:], in_=gate)
+        load_w(1, 0, 2)
+        load_w(1, 2, 2)
+        load_w(1, 4, 1)
+
+        def interleave(engine, dst_ap, src_ap):
+            d = dst_ap.rearrange("p (c i) t -> p c t i", i=4)
+            s = src_ap.rearrange("p t (c i) -> p c t i", i=4)
+            if engine == "s":
+                nc.scalar.copy(d, s)
+            else:
+                nc.vector.tensor_copy(d, s)
+
+        w_bf, w_codes, w_scales = {}, {}, {}
+        for e in range(E):
+            w_bf[e] = keep.tile([P, PASSES, N, 4], BF16, name=f"wbf{e}", align_bytes=64)
+            w_codes[e] = keep.tile([P, PASSES, N], U32, name=f"wcodes{e}", align_bytes=64)
+            w_scales[e] = keep.tile([P, PASSES, N], U8, name=f"wscales{e}", align_bytes=64)
+
+        def w_inter(e, a0, i, shares):
+            for eng, lo, hi in shares:
+                interleave(eng, w_bf[e][:, a0 + i, lo:hi, :], chunks[e, a0][:, i, :, lo:hi])
+
+        def w_quant(e, a, n):
+            nc.vector.quantize_mx(
+                out=w_codes[e][:, a : a + n, :].rearrange("p a n -> p (a n)").bitcast(FP8X4),
+                scales=w_scales[e][:, a : a + n, :].rearrange("p a n -> p (a n)"),
+                in_=w_bf[e][:, a : a + n, :, :].rearrange("p a n j -> p (a n j)"),
+            )
+
+        x_bf = [keep.tile([P, T, 4], BF16, name=f"xbf{a}", align_bytes=64) for a in range(PASSES)]
+        x_codes = keep.tile([P, PASSES * T], U32, name="xcodes", align_bytes=64)
+
+        def place(a):
+            return (PASSES - 1 - a) * T
+        xg = [keep.tile([P, E * C], U32, name=f"xg{a}", align_bytes=64) for a in range(PASSES)]
+
+        def x_inter(a, shares):
+            for eng, lo, hi in shares:
+                for plo, phi, raw in x_raw[a]:
+                    if plo <= lo and hi <= phi:
+                        interleave(eng, x_bf[a][:, lo:hi, :], raw[:, :, lo - plo : hi - plo])
+
+        def x_quant(a, lo, hi):
+            k0 = 4 * max(a - 1, 0)
+            s0 = T if a == 0 else 0
+            nc.vector.quantize_mx(
+                out=x_codes[:, place(a) + lo : place(a) + hi].bitcast(FP8X4),
+                scales=xs[k0:P, s0 + lo : s0 + hi],
+                in_=x_bf[a][:, lo:hi, :].rearrange("p t j -> p (t j)"),
+            )
+
+        def slots(e):
+            return offs_sb[:, e * C // 16 : (e + 1) * C // 16]
+
+        def x_gather(a):
+            if a == 0:
+                for e in range(E):
+                    nc.vector.tensor_copy(
+                        xg[a][:, e * C : (e + 1) * C], x_codes[:, place(a) : place(a) + T].indirect(slots(e))
+                    )
+            else:
+                nc.vector.tensor_copy(xg[a][:], x_codes[:, place(a) : place(a) + 2 * T].indirect(offs_sb[:]))
+
+        def s_gather(b):
+            if b == 0:
+                for e in range(E):
+                    nc.vector.tensor_copy(xg_s[b][:, e * C : (e + 1) * C], xs[:, T : 2 * T].indirect(slots(e)))
+            else:
+                nc.vector.tensor_copy(xg_s[b][:], xs[:].indirect(offs_sb[:]))
+
+        acc = [psum.tile([P, C], F32, name=f"acc{e}") for e in range(E)]
+
+        def mm(e, a):
+            k0 = 4 * max(a - 1, 0)
+            cols = slice(e * C, (e + 1) * C)
+            nc.tensor.matmul_mx(
+                out=acc[e][:],
+                lhsT=w_codes[e][:, a, :].bitcast(FP8X4),
+                lhsT_scale=w_scales[e][:, a, :],
+                rhs=xg[a][:, cols].bitcast(FP8X4),
+                rhs_scale=xg_s[min(a, 1)][k0:P, cols],
+                start=(a == 0),
+                stop=(a == PASSES - 1),
+            )
+
+        out_sb = keep.tile([P, T], F32, name="out_sb")
+        y = keep.tile([P, E * C], F32, name="y")
+
+        def finish(e):
+            cols = slice(e * C, (e + 1) * C)
+            nc.scalar.copy(y[:, cols], acc[e][:])
+            nc.vector.tensor_tensor(
+                out_sb[:].indirect(dst_sb[:, e * C // 16 : (e + 1) * C // 16]), y[:, cols], gate_sb[:, cols], MULT
+            )
+
+        x_inter(0, [("s", 0, 160), ("v", 160, 256)])
+        x_quant(0, 0, 256)
+        x_inter(0, [("s", 256, 416), ("v", 416, 512)])
+        x_quant(0, 256, 512)
+        for a in range(1, PASSES):
+            x_inter(a, [("s", 0, 256), ("s", 256, 512)])
+            x_gather(a - 1)
+            if a == 1:
+                s_gather(0)
+            x_quant(a, 0, 512)
+        x_gather(4)
+        s_gather(1)
+        w_inter(0, 0, 0, [("s", 0, N)])
+        w_inter(0, 0, 1, [("s", 0, N)])
+        w_inter(0, 0, 2, [("s", 0, N)])
+        w_inter(0, 3, 0, [("v", 0, N)])
+        w_inter(0, 3, 1, [("s", 0, N)])
+        w_quant(0, 0, 4)
+        w_quant(0, 4, 1)
+        for a in range(PASSES):
+            mm(0, a)
+        w_inter(1, 0, 0, [("s", 0, N)])
+        w_inter(1, 0, 1, [("s", 0, N)])
+        w_quant(1, 0, 2)
+        finish(0)
+        w_inter(1, 2, 0, [("s", 0, N)])
+        w_inter(1, 2, 1, [("v", 0, N)])
+        w_quant(1, 2, 2)
+        w_inter(1, 4, 0, [("s", 0, 64), ("v", 64, N)])
+        w_quant(1, 4, 1)
+        for a in range(PASSES):
+            mm(1, a)
+        finish(1)
+        nc.sync.dma_start(out=out, in_=out_sb[:])

@@ -13,6 +13,7 @@ U16 = mybir.dt.uint16
 U8 = mybir.dt.uint8
 FP8X4 = mybir.dt.float8_e4m3fn_x4
 MULT = mybir.AluOpType.mult
+ADD = mybir.AluOpType.add
 
 P = 128
 PASSES = K // 512
@@ -71,8 +72,10 @@ def tile_moe_two_lin_none_kernel(tc, xT, w, gate, offs, dst, out):
             s = src_ap.rearrange("p t (c i) -> p c t i", i=4)
             if engine == "s":
                 nc.scalar.copy(d, s)
-            else:
+            elif engine == "v":
                 nc.vector.tensor_copy(d, s)
+            else:
+                nc.gpsimd.tensor_scalar(d, s, 1.0, 0.0, MULT, ADD)
 
         w_bf, w_codes, w_scales = {}, {}, {}
         for e in range(E):
@@ -83,6 +86,12 @@ def tile_moe_two_lin_none_kernel(tc, xT, w, gate, offs, dst, out):
         def w_inter(e, a0, i, shares):
             for eng, lo, hi in shares:
                 interleave(eng, w_bf[e][:, a0 + i, lo:hi, :], chunks[e, a0][:, i, :, lo:hi])
+
+        def w_inter_all(e, a0, i0, i1):
+            nc.scalar.copy(
+                w_bf[e][:, a0 + i0 : a0 + i1, :, :].rearrange("p a (c i) t -> p a c t i", i=4),
+                chunks[e, a0][:, i0:i1, :, :].rearrange("p a t (c i) -> p a c t i", i=4),
+            )
 
         def w_quant(e, a, n):
             nc.vector.quantize_mx(
@@ -162,26 +171,23 @@ def tile_moe_two_lin_none_kernel(tc, xT, w, gate, offs, dst, out):
         x_inter(0, [("s", 256, 416), ("v", 416, 512)])
         x_quant(0, 256, 512)
         for a in range(1, PASSES):
-            x_inter(a, [("s", 0, 256), ("s", 256, 512)])
+            cut = 448 if a < 4 else 320
+            x_inter(a, [("s", 0, cut), ("v", cut, 512)])
             x_gather(a - 1)
             if a == 1:
                 s_gather(0)
             x_quant(a, 0, 512)
         x_gather(4)
         s_gather(1)
-        w_inter(0, 0, 0, [("s", 0, N)])
-        w_inter(0, 0, 1, [("s", 0, N)])
-        w_inter(0, 0, 2, [("s", 0, N)])
-        w_inter(0, 3, 0, [("v", 0, N)])
-        w_inter(0, 3, 1, [("s", 0, N)])
+        w_inter_all(0, 0, 0, 3)
+        w_inter(0, 3, 0, [("s", 0, N)])
+        w_inter(0, 3, 1, [("g", 0, N)])
         w_quant(0, 0, 4)
         w_quant(0, 4, 1)
         for a in range(PASSES):
             mm(0, a)
-        w_inter(1, 0, 0, [("s", 0, N)])
-        w_inter(1, 0, 1, [("s", 0, N)])
+        w_inter_all(1, 0, 0, 2)
         w_quant(1, 0, 2)
-        finish(0)
         w_inter(1, 2, 0, [("s", 0, N)])
         w_inter(1, 2, 1, [("v", 0, N)])
         w_quant(1, 2, 2)
@@ -189,5 +195,6 @@ def tile_moe_two_lin_none_kernel(tc, xT, w, gate, offs, dst, out):
         w_quant(1, 4, 1)
         for a in range(PASSES):
             mm(1, a)
+        finish(0)
         finish(1)
         nc.sync.dma_start(out=out, in_=out_sb[:])

@@ -8,7 +8,6 @@ FLOPS = 2 * K * N * E * C
 F32 = mybir.dt.float32
 BF16 = mybir.dt.bfloat16
 U32 = mybir.dt.uint32
-I32 = mybir.dt.int32
 U16 = mybir.dt.uint16
 U8 = mybir.dt.uint8
 FP8X4 = mybir.dt.float8_e4m3fn_x4
@@ -28,12 +27,19 @@ def tile_moe_two_lin_none_kernel(tc, xT, w, gate, offs, dst, out):
         offs_sb = keep.tile([P, E * C // 16], U16, name="offs_sb")
         dst_sb = keep.tile([P, E * C // 16], U16, name="dst_sb")
         gate_sb = keep.tile([P, E * C], F32, name="gate_sb")
-
         xs = keep.tile([P, 2 * T], U8, name="xs", align_bytes=64)
         nc.gpsimd.memset(xs[:], 0)
         xg_s = [keep.tile([P, E * C], U8, name=f"xgs{b}", align_bytes=64) for b in range(2)]
 
-        chunks = {}
+        x_raw = {}
+        w_raw, w_bf, w_first = {}, {}, {}
+
+        def load_x(a, lo, hi):
+            raw = keep.tile([P, 4, hi - lo], F32, name=f"xraw{a}_{lo}")
+            nc.sync.dma_start(
+                out=raw[:], in_=xT[a * 512 : (a + 1) * 512, lo:hi].rearrange("(p j) t -> p j t", j=4)
+            )
+            x_raw[a, lo] = raw
 
         def load_w(e, a0, n):
             raw = keep.tile([P, n, 4, N], F32, name=f"wraw{e}_{a0}")
@@ -41,31 +47,21 @@ def tile_moe_two_lin_none_kernel(tc, xT, w, gate, offs, dst, out):
                 out=raw[:],
                 in_=w[e, a0 * 512 : (a0 + n) * 512, :].rearrange("(a p j) n -> p a j n", p=P, j=4),
             )
-            chunks[e, a0] = raw
+            w_raw[e, a0] = raw
+            w_bf[e, a0] = keep.tile([P, n, N, 4], BF16, name=f"wbf{e}_{a0}", align_bytes=64, tag="late" if (e, a0) == (1, 2) else f"wbf{e}_{a0}")
 
-        x_raw = []
-
-        def load_x(a, cuts):
-            pieces = []
-            for lo, hi in cuts:
-                raw = keep.tile([P, 4, hi - lo], F32, name=f"xraw{a}_{lo}")
-                nc.sync.dma_start(
-                    out=raw[:], in_=xT[a * 512 : (a + 1) * 512, lo:hi].rearrange("(p j) t -> p j t", j=4)
-                )
-                pieces.append((lo, hi, raw))
-            x_raw.append(pieces)
-
-        load_x(0, [(0, 256), (256, 512)])
+        load_x(0, 0, 256)
+        load_x(0, 256, 512)
         nc.sync.dma_start(offs_sb[:], offs)
         for a in range(1, PASSES):
-            load_x(a, [(0, T)])
-        load_w(0, 0, 3)
-        load_w(0, 3, 2)
-        nc.sync.dma_start(dst_sb[:], dst)
-        nc.sync.dma_start(out=gate_sb[:], in_=gate)
+            load_x(a, 0, T)
+        load_w(0, 0, 4)
+        load_w(0, 4, 1)
         load_w(1, 0, 2)
         load_w(1, 2, 2)
         load_w(1, 4, 1)
+        nc.sync.dma_start(dst_sb[:], dst)
+        nc.sync.dma_start(out=gate_sb[:], in_=gate)
 
         def interleave(engine, dst_ap, src_ap):
             d = dst_ap.rearrange("p (c i) t -> p c t i", i=4)
@@ -77,27 +73,25 @@ def tile_moe_two_lin_none_kernel(tc, xT, w, gate, offs, dst, out):
             else:
                 nc.gpsimd.tensor_scalar(d, s, 1.0, 0.0, MULT, ADD)
 
-        w_bf, w_codes, w_scales = {}, {}, {}
-        for e in range(E):
-            w_bf[e] = keep.tile([P, PASSES, N, 4], BF16, name=f"wbf{e}", align_bytes=64)
-            w_codes[e] = keep.tile([P, PASSES, N], U32, name=f"wcodes{e}", align_bytes=64)
-            w_scales[e] = keep.tile([P, PASSES, N], U8, name=f"wscales{e}", align_bytes=64)
+        def interleave_passes(e, a0, i0, i1):
+            nc.scalar.copy(
+                w_bf[e, a0][:, i0:i1, :, :].rearrange("p a (c i) t -> p a c t i", i=4),
+                w_raw[e, a0][:, i0:i1, :, :].rearrange("p a t (c i) -> p a c t i", i=4),
+            )
 
         def w_inter(e, a0, i, shares):
             for eng, lo, hi in shares:
-                interleave(eng, w_bf[e][:, a0 + i, lo:hi, :], chunks[e, a0][:, i, :, lo:hi])
+                interleave(eng, w_bf[e, a0][:, i, lo:hi, :], w_raw[e, a0][:, i, :, lo:hi])
 
-        def w_inter_all(e, a0, i0, i1):
-            nc.scalar.copy(
-                w_bf[e][:, a0 + i0 : a0 + i1, :, :].rearrange("p a (c i) t -> p a c t i", i=4),
-                chunks[e, a0][:, i0:i1, :, :].rearrange("p a t (c i) -> p a c t i", i=4),
-            )
+        w_codes = [keep.tile([P, PASSES, N], U32, name=f"wcodes{e}", align_bytes=64) for e in range(E)]
+        w_scales = [keep.tile([P, PASSES, N], U8, name=f"wscales{e}", align_bytes=64) for e in range(E)]
 
-        def w_quant(e, a, n):
+        def w_quant(e, a0, i, n):
+            a = a0 + i
             nc.vector.quantize_mx(
                 out=w_codes[e][:, a : a + n, :].rearrange("p a n -> p (a n)").bitcast(FP8X4),
                 scales=w_scales[e][:, a : a + n, :].rearrange("p a n -> p (a n)"),
-                in_=w_bf[e][:, a : a + n, :, :].rearrange("p a n j -> p (a n j)"),
+                in_=w_bf[e, a0][:, i : i + n, :, :].rearrange("p a n j -> p (a n j)"),
             )
 
         x_bf = [keep.tile([P, T, 4], BF16, name=f"xbf{a}", align_bytes=64) for a in range(PASSES)]
@@ -105,13 +99,12 @@ def tile_moe_two_lin_none_kernel(tc, xT, w, gate, offs, dst, out):
 
         def place(a):
             return (PASSES - 1 - a) * T
+
         xg = [keep.tile([P, E * C], U32, name=f"xg{a}", align_bytes=64) for a in range(PASSES)]
 
-        def x_inter(a, shares):
+        def x_inter(a, h, shares):
             for eng, lo, hi in shares:
-                for plo, phi, raw in x_raw[a]:
-                    if plo <= lo and hi <= phi:
-                        interleave(eng, x_bf[a][:, lo:hi, :], raw[:, :, lo - plo : hi - plo])
+                interleave(eng, x_bf[a][:, h + lo : h + hi, :], x_raw[a, h][:, :, lo:hi])
 
         def x_quant(a, lo, hi):
             k0 = 4 * max(a - 1, 0)
@@ -157,42 +150,46 @@ def tile_moe_two_lin_none_kernel(tc, xT, w, gate, offs, dst, out):
             )
 
         out_sb = keep.tile([P, T], F32, name="out_sb")
-        y = keep.tile([P, E * C], F32, name="y")
 
         def finish(e):
-            cols = slice(e * C, (e + 1) * C)
-            nc.scalar.copy(y[:, cols], acc[e][:])
+            y = keep.tile([P, C], F32, name=f"y{e}", tag="late" if e == 0 else "y1", align_bytes=64)
+            nc.scalar.copy(y[:], acc[e][:])
             nc.vector.tensor_tensor(
-                out_sb[:].indirect(dst_sb[:, e * C // 16 : (e + 1) * C // 16]), y[:, cols], gate_sb[:, cols], MULT
+                out_sb[:].indirect(dst_sb[:, e * C // 16 : (e + 1) * C // 16]),
+                y[:],
+                gate_sb[:, e * C : (e + 1) * C],
+                MULT,
             )
 
-        x_inter(0, [("s", 0, 160), ("v", 160, 256)])
+        x_inter(0, 0, [("s", 0, 160), ("v", 160, 256)])
         x_quant(0, 0, 256)
-        x_inter(0, [("s", 256, 416), ("v", 416, 512)])
+        x_inter(0, 256, [("s", 0, 160), ("v", 160, 256)])
         x_quant(0, 256, 512)
         for a in range(1, PASSES):
-            cut = 448 if a < 4 else 320
-            x_inter(a, [("s", 0, cut), ("v", cut, 512)])
-            x_gather(a - 1)
+            cut = 448 if a < 4 else 352
             if a == 1:
+                x_gather(0)
                 s_gather(0)
+            x_inter(a, 0, [("s", 0, cut), ("v", cut, 512)])
+            if a > 1:
+                x_gather(a - 1)
             x_quant(a, 0, 512)
         x_gather(4)
         s_gather(1)
-        w_inter_all(0, 0, 0, 3)
-        w_inter(0, 3, 0, [("s", 0, N)])
-        w_inter(0, 3, 1, [("g", 0, N)])
-        w_quant(0, 0, 4)
-        w_quant(0, 4, 1)
+        interleave_passes(0, 0, 0, 3)
+        w_inter(0, 0, 3, [("g", 0, N)])
+        w_inter(0, 4, 0, [("s", 0, N)])
+        w_quant(0, 0, 0, 4)
+        w_quant(0, 4, 0, 1)
         for a in range(PASSES):
             mm(0, a)
-        w_inter_all(1, 0, 0, 2)
-        w_quant(1, 0, 2)
+        interleave_passes(1, 0, 0, 2)
+        w_quant(1, 0, 0, 2)
         w_inter(1, 2, 0, [("s", 0, N)])
         w_inter(1, 2, 1, [("v", 0, N)])
-        w_quant(1, 2, 2)
+        w_quant(1, 2, 0, 2)
         w_inter(1, 4, 0, [("s", 0, 64), ("v", 64, N)])
-        w_quant(1, 4, 1)
+        w_quant(1, 4, 0, 1)
         for a in range(PASSES):
             mm(1, a)
         finish(0)

@@ -48,10 +48,9 @@ def tile_moe_two_lin_none_kernel(tc, xT, w, gate, offs, dst, out):
                 in_=w[e, a0 * 512 : (a0 + n) * 512, :].rearrange("(a p j) n -> p a j n", p=P, j=4),
             )
             w_raw[e, a0] = raw
-            w_bf[e, a0] = keep.tile([P, n, N, 4], BF16, name=f"wbf{e}_{a0}", align_bytes=64, tag="late" if (e, a0) == (1, 2) else f"wbf{e}_{a0}")
+            w_bf[e, a0] = keep.tile([P, n, N, 4], BF16, name=f"wbf{e}_{a0}", align_bytes=64)
 
-        load_x(0, 0, 256)
-        load_x(0, 256, 512)
+        load_x(0, 0, T)
         nc.sync.dma_start(offs_sb[:], offs)
         for a in range(1, PASSES):
             load_x(a, 0, T)
@@ -127,12 +126,10 @@ def tile_moe_two_lin_none_kernel(tc, xT, w, gate, offs, dst, out):
             else:
                 nc.vector.tensor_copy(xg[a][:], x_codes[:, place(a) : place(a) + 2 * T].indirect(offs_sb[:]))
 
-        def s_gather(b):
-            if b == 0:
-                for e in range(E):
-                    nc.vector.tensor_copy(xg_s[b][:, e * C : (e + 1) * C], xs[:, T : 2 * T].indirect(slots(e)))
-            else:
-                nc.vector.tensor_copy(xg_s[b][:], xs[:].indirect(offs_sb[:]))
+        def s_gather(b, experts):
+            first = T if b == 0 else 0
+            for e in experts:
+                nc.vector.tensor_copy(xg_s[b][:, e * C : (e + 1) * C], xs[:, first : first + T].indirect(slots(e)))
 
         acc = [psum.tile([P, C], F32, name=f"acc{e}") for e in range(E)]
 
@@ -152,7 +149,7 @@ def tile_moe_two_lin_none_kernel(tc, xT, w, gate, offs, dst, out):
         out_sb = keep.tile([P, T], F32, name="out_sb")
 
         def finish(e):
-            y = keep.tile([P, C], F32, name=f"y{e}", tag="late" if e == 0 else "y1", align_bytes=64)
+            y = keep.tile([P, C], F32, name=f"y{e}", align_bytes=64)
             nc.scalar.copy(y[:], acc[e][:])
             nc.vector.tensor_tensor(
                 out_sb[:].indirect(dst_sb[:, e * C // 16 : (e + 1) * C // 16]),
@@ -161,32 +158,34 @@ def tile_moe_two_lin_none_kernel(tc, xT, w, gate, offs, dst, out):
                 MULT,
             )
 
-        x_inter(0, 0, [("s", 0, 160), ("v", 160, 256)])
-        x_quant(0, 0, 256)
-        x_inter(0, 256, [("s", 0, 160), ("v", 160, 256)])
-        x_quant(0, 256, 512)
-        for a in range(1, PASSES):
-            cut = 448 if a < 4 else 352
-            if a == 1:
-                x_gather(0)
-                s_gather(0)
-            x_inter(a, 0, [("s", 0, cut), ("v", cut, 512)])
-            if a > 1:
-                x_gather(a - 1)
-            x_quant(a, 0, 512)
-        x_gather(4)
-        s_gather(1)
+        x_inter(0, 0, [("s", 0, 256), ("v", 256, 512)])
+        x_quant(0, 0, 512)
+        x_gather(0)
+        s_gather(0, [0, 1])
+        x_inter(1, 0, [("s", 0, 448), ("v", 448, 512)])
+        x_quant(1, 0, 512)
+        x_gather(1)
+        x_inter(2, 0, [("s", 0, 416), ("v", 416, 512)])
+        x_quant(2, 0, 512)
+        x_gather(2)
+        x_inter(3, 0, [("s", 0, 416), ("v", 416, 512)])
+        x_quant(3, 0, 512)
+        x_inter(4, 0, [("s", 0, 384), ("v", 384, 512)])
+        x_gather(3)
+        x_quant(4, 0, 512)
         interleave_passes(0, 0, 0, 3)
         w_inter(0, 0, 3, [("g", 0, N)])
         w_inter(0, 4, 0, [("s", 0, N)])
+        x_gather(4)
+        s_gather(1, [0])
         w_quant(0, 0, 0, 4)
         w_quant(0, 4, 0, 1)
+        s_gather(1, [1])
         for a in range(PASSES):
             mm(0, a)
         interleave_passes(1, 0, 0, 2)
         w_quant(1, 0, 0, 2)
-        w_inter(1, 2, 0, [("s", 0, N)])
-        w_inter(1, 2, 1, [("v", 0, N)])
+        interleave_passes(1, 2, 0, 2)
         w_quant(1, 2, 0, 2)
         w_inter(1, 4, 0, [("s", 0, 64), ("v", 64, N)])
         w_quant(1, 4, 0, 1)

from contextlib import ExitStack

import concourse.mybir as mybir

K, T, E, C, N = 2560, 512, 2, 256, 128
FLOPS = 2 * K * N * E * C

F32 = mybir.dt.float32
BF16 = mybir.dt.bfloat16
U32 = mybir.dt.uint32
U16 = mybir.dt.uint16
U8 = mybir.dt.uint8
FP8X4 = mybir.dt.float8_e4m3fn_x4
MULT = mybir.AluOpType.mult
ADD = mybir.AluOpType.add

P = 128
PASSES = K // 512


def tile_moe_two_lin_none_kernel(tc, xT, w, gate, offs, dst, out):
    nc = tc.nc
    with ExitStack() as ctx:
        keep = ctx.enter_context(tc.tile_pool(name="keep", bufs=1))
        psum = ctx.enter_context(tc.psum_pool(name="psum", bufs=1))

        offs_sb = keep.tile([P, E * C // 16], U16, name="offs_sb")
        dst_sb = keep.tile([P, E * C // 16], U16, name="dst_sb")
        gate_sb = keep.tile([P, E * C], F32, name="gate_sb")
        xs = keep.tile([P, 2 * T], U8, name="xs", align_bytes=64)
        nc.gpsimd.memset(xs[:], 0)
        xg_s = [keep.tile([P, E * C], U8, name=f"xgs{b}", align_bytes=64) for b in range(2)]

        x_raw = {}
        w_raw, w_bf, w_first = {}, {}, {}

        def load_x(a, lo, hi):
            raw = keep.tile([P, 4, hi - lo], F32, name=f"xraw{a}_{lo}")
            nc.sync.dma_start(
                out=raw[:], in_=xT[a * 512 : (a + 1) * 512, lo:hi].rearrange("(p j) t -> p j t", j=4)
            )
            x_raw[a, lo] = raw

        def load_w(e, a0, n):
            raw = keep.tile([P, n, 4, N], F32, name=f"wraw{e}_{a0}")
            nc.sync.dma_start(
                out=raw[:],
                in_=w[e, a0 * 512 : (a0 + n) * 512, :].rearrange("(a p j) n -> p a j n", p=P, j=4),
            )
            w_raw[e, a0] = raw
            w_bf[e, a0] = keep.tile([P, n, N, 4], BF16, name=f"wbf{e}_{a0}", align_bytes=64)

        load_x(0, 0, T)
        nc.sync.dma_start(offs_sb[:], offs)
        for a in range(1, PASSES):
            load_x(a, 0, T)
        load_w(0, 0, 4)
        load_w(0, 4, 1)
        load_w(1, 0, 2)
        load_w(1, 2, 2)
        load_w(1, 4, 1)
        nc.sync.dma_start(dst_sb[:], dst)
        nc.sync.dma_start(out=gate_sb[:], in_=gate)

        def interleave(engine, dst_ap, src_ap):
            d = dst_ap.rearrange("p (c i) t -> p c t i", i=4)
            s = src_ap.rearrange("p t (c i) -> p c t i", i=4)
            if engine == "s":
                nc.scalar.copy(d, s)
            elif engine == "v":
                nc.vector.tensor_copy(d, s)
            else:
                nc.gpsimd.tensor_scalar(d, s, 1.0, 0.0, MULT, ADD)

        def interleave_passes(e, a0, i0, i1):
            nc.scalar.copy(
                w_bf[e, a0][:, i0:i1, :, :].rearrange("p a (c i) t -> p a c t i", i=4),
                w_raw[e, a0][:, i0:i1, :, :].rearrange("p a t (c i) -> p a c t i", i=4),
            )

        def w_inter(e, a0, i, shares):
            for eng, lo, hi in shares:
                interleave(eng, w_bf[e, a0][:, i, lo:hi, :], w_raw[e, a0][:, i, :, lo:hi])

        w_codes = [keep.tile([P, PASSES, N], U32, name=f"wcodes{e}", align_bytes=64) for e in range(E)]
        w_scales = [keep.tile([P, PASSES, N], U8, name=f"wscales{e}", align_bytes=64) for e in range(E)]

        def w_quant(e, a0, i, n):
            a = a0 + i
            nc.vector.quantize_mx(
                out=w_codes[e][:, a : a + n, :].rearrange("p a n -> p (a n)").bitcast(FP8X4),
                scales=w_scales[e][:, a : a + n, :].rearrange("p a n -> p (a n)"),
                in_=w_bf[e, a0][:, i : i + n, :, :].rearrange("p a n j -> p (a n j)"),
            )

        x_bf = [keep.tile([P, T, 4], BF16, name=f"xbf{a}", align_bytes=64) for a in range(PASSES)]
        x_codes = keep.tile([P, PASSES * T], U32, name="xcodes", align_bytes=64)

        def place(a):
            return (PASSES - 1 - a) * T

        xg = [keep.tile([P, E * C], U32, name=f"xg{a}", align_bytes=64) for a in range(PASSES)]

        def x_inter(a, h, shares):
            for eng, lo, hi in shares:
                interleave(eng, x_bf[a][:, h + lo : h + hi, :], x_raw[a, h][:, :, lo:hi])

        def x_quant(a, lo, hi):
            k0 = 4 * max(a - 1, 0)
            s0 = T if a == 0 else 0
            nc.vector.quantize_mx(
                out=x_codes[:, place(a) + lo : place(a) + hi].bitcast(FP8X4),
                scales=xs[k0:P, s0 + lo : s0 + hi],
                in_=x_bf[a][:, lo:hi, :].rearrange("p t j -> p (t j)"),
            )

        def slots(e):
            return offs_sb[:, e * C // 16 : (e + 1) * C // 16]

        def x_gather(a):
            if a == 0:
                for e in range(E):
                    nc.vector.tensor_copy(
                        xg[a][:, e * C : (e + 1) * C], x_codes[:, place(a) : place(a) + T].indirect(slots(e))
                    )
            else:
                nc.vector.tensor_copy(xg[a][:], x_codes[:, place(a) : place(a) + 2 * T].indirect(offs_sb[:]))

        def s_gather(b, experts):
            first = T if b == 0 else 0
            for e in experts:
                nc.vector.tensor_copy(xg_s[b][:, e * C : (e + 1) * C], xs[:, first : first + T].indirect(slots(e)))

        acc = [psum.tile([P, C], F32, name=f"acc{e}") for e in range(E)]

        def mm(e, a):
            k0 = 4 * max(a - 1, 0)
            cols = slice(e * C, (e + 1) * C)
            nc.tensor.matmul_mx(
                out=acc[e][:],
                lhsT=w_codes[e][:, a, :].bitcast(FP8X4),
                lhsT_scale=w_scales[e][:, a, :],
                rhs=xg[a][:, cols].bitcast(FP8X4),
                rhs_scale=xg_s[min(a, 1)][k0:P, cols],
                start=(a == 0),
                stop=(a == PASSES - 1),
            )

        out_sb = keep.tile([P, T], F32, name="out_sb")

        def finish(e):
            y = keep.tile([P, C], F32, name=f"y{e}", align_bytes=64)
            nc.scalar.copy(y[:], acc[e][:])
            nc.vector.tensor_tensor(
                out_sb[:].indirect(dst_sb[:, e * C // 16 : (e + 1) * C // 16]),
                y[:],
                gate_sb[:, e * C : (e + 1) * C],
                MULT,
            )

        x_inter(0, 0, [("s", 0, 256), ("v", 256, 512)])
        x_quant(0, 0, 512)
        x_gather(0)
        s_gather(0, [0, 1])
        x_inter(1, 0, [("s", 0, 448), ("v", 448, 512)])
        x_quant(1, 0, 512)
        x_gather(1)
        x_inter(2, 0, [("s", 0, 416), ("v", 416, 512)])
        x_quant(2, 0, 512)
        x_gather(2)
        x_inter(3, 0, [("s", 0, 416), ("v", 416, 512)])
        x_quant(3, 0, 512)
        x_inter(4, 0, [("s", 0, 384), ("v", 384, 512)])
        x_gather(3)
        x_quant(4, 0, 512)
        interleave_passes(0, 0, 0, 3)
        w_inter(0, 0, 3, [("g", 0, N)])
        w_inter(0, 4, 0, [("s", 0, N)])
        x_gather(4)
        s_gather(1, [0])
        w_quant(0, 0, 0, 4)
        w_quant(0, 4, 0, 1)
        s_gather(1, [1])
        for a in range(PASSES):
            mm(0, a)
        interleave_passes(1, 0, 0, 2)
        w_quant(1, 0, 0, 2)
        interleave_passes(1, 2, 0, 2)
        w_quant(1, 2, 0, 2)
        w_inter(1, 4, 0, [("s", 0, 64), ("v", 64, N)])
        w_quant(1, 4, 0, 1)
        for a in range(PASSES):
            mm(1, a)
        finish(0)
        finish(1)
        nc.sync.dma_start(out=out, in_=out_sb[:])
